import numpy as np
import ml_dtypes


def mxq(x, axis, fmt="e4m3"):
    dtype, down = {"e4m3": (ml_dtypes.float8_e4m3fn, 7), "e5m2": (ml_dtypes.float8_e5m2, 14)}[fmt]
    v = np.moveaxis(np.asarray(x, np.float32).astype(ml_dtypes.bfloat16).astype(np.float64), axis, -1)
    blocks = v.reshape(v.shape[:-1] + (-1, 32))
    amax = np.abs(blocks).max(-1, keepdims=True)
    byte = np.maximum(np.where(amax > 0, np.frexp(amax)[1] - 1 + 127, 0) - down, 1)
    scale = np.exp2(byte - 127.0)
    codes = (blocks / scale).astype(np.float32).astype(dtype).astype(np.float64)
    return np.moveaxis((codes * scale).reshape(v.shape), -1, axis)


WIDE = False


def mx_kscale(k):
    if not WIDE:
        return np.ones(k)
    levels = np.array([10, -10, 5, -5, 0])
    if k % 512:
        return np.exp2(np.random.permutation(np.resize(levels, k // 32))).repeat(32)
    a = np.empty((k // 512, 16))
    for p in range(k // 512):
        a[p, :8] = np.random.permutation(np.resize(levels, 8))
        for g in range(8):
            far = levels[np.abs(levels - a[p, g]) >= 10]
            a[p, g + 8] = far[np.random.randint(len(far))]
    return np.exp2(a.ravel()).repeat(32)


def f64(x):
    return np.asarray(x).astype(np.float64)


def striped(idx):
    return np.tile(idx.reshape(-1, 16).T, (8, 1)).astype(np.uint16)


def unstriped(offs):
    return offs[:16].T.reshape(-1).astype(np.int64)


def striped8(idx):
    return np.concatenate([x.reshape(-1, 16).T for x in idx]).astype(np.uint16)


def runs(offs, k):
    lists = np.stack([offs[16 * r : 16 * r + 16].T.reshape(-1) for r in range(8)]).astype(np.int64)
    return lists[np.arange(k) % 512 // 64]


def pack_weight(w):
    k, n = w.shape
    w = f64(np.asarray(w, np.float32).astype(ml_dtypes.bfloat16)).reshape(k // 32, 32, n)
    amax = np.abs(w).max(1)
    byte = np.clip(np.where(amax > 0, np.frexp(amax)[1] - 1 + 127 - 7, 1), 1, 254)
    scaled = (w * np.exp2(127.0 - byte)[:, None, :]).reshape(k, n).astype(np.float32)
    words = np.ascontiguousarray(scaled.reshape(k // 512, 128, 4, n).transpose(0, 1, 3, 2)).astype(ml_dtypes.float8_e4m3fn).view(np.uint8)
    return words, np.ascontiguousarray(byte.astype(np.uint8).reshape(k // 512, 16, n))


def unpack_weight(words, scales):
    g, p, n, _ = words.shape
    vals = np.ascontiguousarray(words).view(ml_dtypes.float8_e4m3fn).astype(np.float64) * np.repeat(np.exp2(scales.astype(np.float64) - 127.0), 8, axis=1)[..., None]
    return vals.transpose(0, 1, 3, 2).reshape(g * 512, n)


E2M1 = np.array([0.0, 0.5, 1.0, 1.5, 2.0, 3.0, 4.0, 6.0, -0.0, -0.5, -1.0, -1.5, -2.0, -3.0, -4.0, -6.0])


def pack_fp4(w):
    k, n = w.shape
    w = f64(np.asarray(w, np.float32).astype(ml_dtypes.bfloat16)).reshape(k // 32, 32, n)
    amax = np.abs(w).max(1)
    mant, ex = np.frexp(amax / 6.0)
    byte = np.clip(np.where(amax > 0, np.where(mant > 0.5, ex, ex - 1) + 127, 1), 1, 254)
    scaled = (w * np.exp2(127.0 - byte)[:, None, :]).reshape(k, n).astype(np.float32)
    c = np.ascontiguousarray(scaled.reshape(k // 512, 128, 4, n).transpose(0, 1, 3, 2)).astype(ml_dtypes.float4_e2m1fn).view(np.uint8) & 0xF
    words = (c[..., 0::2] | (c[..., 1::2] << 4)).reshape(k // 512, 128, 2 * n)
    return np.ascontiguousarray(words), np.ascontiguousarray(byte.astype(np.uint8).reshape(k // 512, 16, n))


def unpack_fp4(words, scales):
    g, _, n = scales.shape
    words = np.ascontiguousarray(words).reshape(g, 128, n, 2)
    nib = np.empty((g, 128, n, 4), np.uint8)
    nib[..., 0::2] = words & 0xF
    nib[..., 1::2] = words >> 4
    vals = E2M1[nib] * np.repeat(np.exp2(scales.astype(np.float64) - 127.0), 8, axis=1)[..., None]
    return vals.transpose(0, 1, 3, 2).reshape(g * 512, n)


def relu(v):
    return np.maximum(v, 0.0)

def planes(y):
    n, m = y.shape
    v = y.astype(np.float32).astype(ml_dtypes.bfloat16).astype(np.float64).reshape(n // 32, 32, m)
    top = np.abs(v).max(1)
    byte = np.clip(np.where(top > 0, np.frexp(top)[1] - 1 + 127 - 7, 1), 1, 254)
    codes = (v * np.exp2(127.0 - byte)[:, None, :]).reshape(n, m).astype(np.float32).astype(ml_dtypes.float8_e4m3fn).view(np.uint8)
    words = codes.reshape(n // 512, 128, 4, m).transpose(0, 1, 3, 2)
    return np.ascontiguousarray(words), np.ascontiguousarray(byte.astype(np.uint8).reshape(n // 512, 16, m))


K, T, S, H, C = 512, 2048, 256, 512, 512


def setup_inputs():
    n = np.random.standard_normal
    s = mx_kscale(K)[:, None]
    packed_xT = pack_weight(n((K, T)) * s)
    packed_w1 = pack_fp4(n((K, H)) / np.sqrt(K) / s)
    packed_w2 = pack_fp4(n((K, H)) / np.sqrt(K) / s)
    return {
        "x_words": packed_xT[0],
        "x_scales": packed_xT[1],
        "w1_words": packed_w1[0],
        "w1_scales": packed_w1[1],
        "w2_words": packed_w2[0],
        "w2_scales": packed_w2[1],
        "gs": (np.random.uniform(0.5, 1.5, (K, 1)) / s).astype(np.float32),
        "offs": striped(np.random.permutation(T)[:S]),
        "two": striped(np.random.permutation(T)[:S]),
        "n1": striped8(np.stack([np.random.permutation(S) for _ in range(8)])),
        "n2": striped8(np.stack([np.random.permutation(S) for _ in range(8)])),
        "cand": striped(np.random.permutation(T)[:C]),
        "n3": striped8(np.stack([np.random.permutation(S) for _ in range(8)])),
        "n4": striped8(np.stack([np.random.permutation(S) for _ in range(8)])),
    }


def reference(x_words, x_scales, w1_words, w1_scales, w2_words, w2_scales, gs, offs, two, n1, n2, cand, n3, n4):
    x_cand = unpack_weight(x_words, x_scales)[:, unstriped(cand)]
    xq = unpack_weight(x_words, x_scales)[:, unstriped(offs)]
    y = unpack_fp4(w1_words, w1_scales).T @ xq
    x_two = unpack_weight(x_words, x_scales)[:, unstriped(two)]
    d = unpack_fp4(w2_words, w2_scales).T @ x_two
    z = f64(gs) * (y * (np.tanh(d[np.arange(H)[:, None], runs(n1, H)] - (d[np.arange(H)[:, None], runs(n2, H)]))))
    s = 0.0625 * ((x_cand.T @ mxq(z, 0, "e4m3")))
    pa = s - (s[np.arange(C)[:, None], runs(n3, C)])
    pb = s[np.arange(C)[:, None], runs(n4, C)] - s
    out_0 = relu(np.minimum(pa, pb)) - (relu(-1.0 * np.maximum(pa, pb)))
    return (out_0,) + planes(out_0)

@@ -1,0 +1,230 @@
+from contextlib import ExitStack
+
+import concourse.mybir as mybir
+
+F32 = mybir.dt.float32
+BF16 = mybir.dt.bfloat16
+I32 = mybir.dt.int32
+U32 = mybir.dt.uint32
+U16 = mybir.dt.uint16
+U8 = mybir.dt.uint8
+FP8X4 = mybir.dt.float8_e4m3fn_x4
+FP4X4 = mybir.dt.float4_e2m1fn_x4
+ACT = mybir.ActivationFunctionType
+ALU = mybir.AluOpType
+
+P = 128
+K, T, S, H, C = 512, 2048, 256, 512, 512
+PACK = 4
+HALF = 128
+FLOPS = 2 * K * (H * S + H * S + C * S)
+
+
+def tile_picked_twcjointbminmod_none_po_kernel(tc, x_words, x_scales, w1_words, w1_scales, w2_words, w2_scales, gs, offs, two, n1, n2, cand, n3, n4, out_0, out_1, out_2):
+    nc = tc.nc
+    with ExitStack() as ctx:
+        sb = ctx.enter_context(tc.tile_pool(name="sb", bufs=1))
+        ps = ctx.enter_context(tc.psum_pool(name="ps", bufs=1))
+
+        def load_list(src, name):
+            t = sb.tile([P, src.shape[1]], U16, name=name)
+            nc.sync.dma_start(t[:], src)
+            return t
+
+        def load_scales(queues, dst, src):
+            for q, queue in enumerate(queues):
+                queue.dma_start(dst[32 * q : 32 * q + 4, :].bitcast(I32), src[0, 4 * q : 4 * q + 4, :].bitcast(I32))
+
+        xs = sb.tile([P, T], U8, name="xs", align_bytes=64)
+        w2s_raw = sb.tile([P, H], U8, name="w2s_raw", align_bytes=64)
+        w1s_raw = sb.tile([P, H], U8, name="w1s_raw", align_bytes=64)
+        nc.vector.memset(xs[:].bitcast(I32), 0)
+        nc.gpsimd.memset(w2s_raw[:].bitcast(I32), 0)
+        nc.vector.memset(w1s_raw[:].bitcast(I32), 0)
+
+        xw = sb.tile([P, T], U32, name="xw", align_bytes=64)
+        w2w_raw = sb.tile([P, 2 * H], U8, name="w2w_raw", align_bytes=64)
+        w1w_raw = sb.tile([P, 2 * H], U8, name="w1w_raw", align_bytes=64)
+        gs_sb = sb.tile([P, PACK], F32, name="gs_sb")
+
+        load_scales([nc.scalar] * 4, xs, x_scales)
+        two_sb = load_list(two, "two_sb")
+        nc.sync.dma_start(w2w_raw[:].bitcast(I32), w2_words[0].bitcast(I32))
+        cand_sb = load_list(cand, "cand_sb")
+        nc.sync.dma_start(xw[:].bitcast(I32), x_words[0].rearrange("p c r -> p (c r)").bitcast(I32))
+        load_scales([nc.gpsimd, nc.gpsimd, nc.scalar, nc.scalar], w2s_raw, w2_scales)
+        n1_sb = load_list(n1, "n1_sb")
+        n2_sb = load_list(n2, "n2_sb")
+        offs_sb = load_list(offs, "offs_sb")
+        nc.sync.dma_start(w1w_raw[:].bitcast(I32), w1_words[0].bitcast(I32))
+        load_scales([nc.sync] * 4, w1s_raw, w1_scales)
+        nc.sync.dma_start(gs_sb[:], gs.rearrange("(p t) o -> p (t o)", t=PACK))
+        n4_sb = load_list(n4, "n4_sb")
+        n3_sb = load_list(n3, "n3_sb")
+
+        def deal(src, width, dtype, name, per):
+            dst = sb.tile([P, width * per], dtype, name=name, align_bytes=64)
+            nc.vector.tensor_copy(
+                dst[:].rearrange("p (t m b) -> p t m b", t=PACK, b=per),
+                src[:].rearrange("p (m t b) -> p t m b", t=PACK, b=per),
+            )
+            return dst
+
+        def deal16(src, name):
+            dst = sb.tile([P, 2 * H], U8, name=name, align_bytes=64)
+            nc.vector.tensor_copy(
+                dst[:].bitcast(U16).rearrange("p (t m) -> p t m", t=PACK),
+                src[:].bitcast(U16).rearrange("p (m t) -> p t m", t=PACK),
+            )
+            return dst
+
+        def pick(table, lst, dtype, name, pieces=1):
+            n = lst.shape[1] * 16
+            dst = sb.tile([P, n], dtype, name=name, align_bytes=64)
+            step = n // pieces
+            for a in range(0, n, step):
+                nc.vector.tensor_copy(dst[:, a : a + step], table[:].indirect(lst[:, a // 16 : (a + step) // 16]))
+            return dst
+
+        w2w = deal16(w2w_raw, "w2w")
+        two_s = pick(xs, two_sb, U8, "two_s")
+        cand_s = deal(pick(xs, cand_sb, U8, "cand_s_raw", 2), C, U8, "cand_s", 1)
+        w2s = deal(w2s_raw, H, U8, "w2s", 1)
+        two_w = pick(xw, two_sb, U32, "two_w")
+
+        def first_product(bank, ww, ws, t, tok_w, tok_s):
+            nc.tensor.matmul_mx(
+                out=bank,
+                lhsT=ww[:, 2 * P * t : 2 * P * (t + 1)].bitcast(FP4X4),
+                lhsT_scale=ws[:, P * t : P * (t + 1)],
+                rhs=tok_w[:].bitcast(FP8X4),
+                rhs_scale=tok_s[:],
+                start=True,
+                stop=True,
+            )
+
+        d_sb = []
+        for t in range(PACK):
+            bank = ps.tile([P, S], F32, name=f"d_ps{t}", tag=f"row{t}")
+            first_product(bank[:], w2w, w2s, t, two_w, two_s)
+            d_t = sb.tile([P, S], F32, name=f"d{t}")
+            if t == 0:
+                nc.scalar.activation(d_t[:], bank[:], ACT.Copy)
+            else:
+                nc.vector.tensor_copy(d_t[:], bank[:])
+            d_sb.append(d_t)
+
+        cand_w = deal(pick(xw, cand_sb, U32, "cand_w_raw", 2), C, U32, "cand_w", 1)
+        offs_s = pick(xs, offs_sb, U8, "offs_s")
+        offs_w = pick(xw, offs_sb, U32, "offs_w")
+        w1w = deal16(w1w_raw, "w1w")
+        w1s = deal(w1s_raw, H, U8, "w1s", 1)
+        y_ps = [ps.tile([P, 2, S], F32, name=f"y_ps{u}") for u in range(2)]
+        for t in range(PACK):
+            first_product(y_ps[t // 2][:, t % 2, :], w1w, w1s, t, offs_w, offs_s)
+
+        halves = [slice(h * HALF, (h + 1) * HALF) for h in range(S // HALF)]
+        cols16 = [slice(h * HALF // 16, (h + 1) * HALF // 16) for h in range(S // HALF)]
+
+        g1 = [sb.tile([P, PACK, HALF], F32, name=f"g1_{h}") for h in range(2)]
+        g2 = [sb.tile([P, PACK, HALF], F32, name=f"g2_{h}") for h in range(2)]
+        df = [sb.tile([P, PACK, HALF], F32, name=f"df_{h}") for h in range(2)]
+        th = [sb.tile([P, PACK, HALF], F32, name=f"th_{h}") for h in range(2)]
+        zb = [sb.tile([P, PACK, HALF], BF16, name=f"zb_{h}", align_bytes=64) for h in range(2)]
+        zi = [sb.tile([P, HALF, PACK], BF16, name=f"zi_{h}", align_bytes=64) for h in range(2)]
+        zw = [sb.tile([P, HALF], U32, name=f"zw_{h}", align_bytes=64) for h in range(2)]
+        zs = [sb.tile([P, HALF], U8, name=f"zs_{h}", align_bytes=64) for h in range(2)]
+
+        def fetch_d(h, t):
+            nc.scalar.activation(g1[h][:, t, :], d_sb[t][:].indirect(n1_sb[:, cols16[h]]), ACT.Copy)
+            nc.scalar.activation(g2[h][:, t, :], d_sb[t][:].indirect(n2_sb[:, cols16[h]]), ACT.Copy)
+            nc.vector.tensor_tensor(df[h][:, t, :], g1[h][:, t, :], g2[h][:, t, :], ALU.subtract)
+
+        def gate(h, t):
+            nc.scalar.activation(th[h][:, t, :], df[h][:, t, :], ACT.Tanh)
+            nc.vector.scalar_tensor_tensor(
+                zb[h][:, t, :], y_ps[t // 2][:, t % 2, halves[h]], gs_sb[:, t : t + 1], th[h][:, t, :], ALU.mult, ALU.mult
+            )
+
+        def quantise_z(h):
+            nc.vector.tensor_copy(zi[h][:], zb[h][:].rearrange("p t j -> p j t"))
+            nc.vector.quantize_mx(out=zw[h][:].bitcast(FP8X4), scales=zs[h][:], in_=zi[h][:].rearrange("p j t -> p (j t)"))
+
+        steps = [(h, t) for h in range(2) for t in range(PACK)]
+        fetch_d(*steps[0])
+
+        s_sb = [sb.tile([P, S], F32, name=f"s{t}") for t in range(PACK)]
+        s_first = ps.tile([P, PACK, HALF], F32, name="s_first")
+
+        def score(h):
+            for t in range(PACK):
+                bank = s_first[:, t, :] if h == 0 else ps.tile([P, S], F32, name=f"s_ps{t}", tag=f"row{t}")[:, 0:HALF]
+                nc.tensor.matmul_mx(
+                    out=bank,
+                    lhsT=cand_w[:, P * t : P * (t + 1)].bitcast(FP8X4),
+                    lhsT_scale=cand_s[:, P * t : P * (t + 1)],
+                    rhs=zw[h][:].bitcast(FP8X4),
+                    rhs_scale=zs[h][:],
+                    start=True,
+                    stop=True,
+                )
+                if h == 1:
+                    if t == 0:
+                        nc.scalar.activation(s_sb[t][:, halves[h]], bank, ACT.Copy, scale=0.0625)
+                    else:
+                        nc.vector.tensor_scalar_mul(s_sb[t][:, halves[h]], bank, 0.0625)
+
+        for i in range(1, len(steps)):
+            fetch_d(*steps[i])
+            gate(*steps[i - 1])
+            if steps[i - 1] == (0, PACK - 1):
+                quantise_z(0)
+                score(0)
+        gate(*steps[-1])
+        quantise_z(1)
+        for t in range(PACK):
+            nc.scalar.activation(s_sb[t][:, halves[0]], s_first[:, t, :], ACT.Copy, scale=0.0625)
+        score(1)
+
+        ga = [sb.tile([P, PACK, HALF], F32, name=f"ga_{h}") for h in range(2)]
+        gb = [sb.tile([P, PACK, HALF], F32, name=f"gb_{h}") for h in range(2)]
+        pa = [sb.tile([P, PACK, HALF], F32, name=f"pa_{h}") for h in range(2)]
+        pb = [sb.tile([P, PACK, HALF], F32, name=f"pb_{h}") for h in range(2)]
+        up = [sb.tile([P, PACK, HALF], F32, name=f"up_{h}") for h in range(2)]
+        res = [sb.tile([P, PACK, HALF], F32, name=f"res_{h}") for h in range(2)]
+        ri = [sb.tile([P, HALF, PACK], BF16, name=f"ri_{h}", align_bytes=64) for h in range(2)]
+        rw = [sb.tile([P, HALF], U32, name=f"rw_{h}", align_bytes=64) for h in range(2)]
+        rs = sb.tile([P, S], U8, name="rs", align_bytes=64)
+        out_rows = out_0.rearrange("(p t) j -> p t j", t=PACK)
+        out_words = out_1[0].rearrange("p c r -> p (c r)").bitcast(I32)
+
+        def fetch_s(h, t):
+            nc.scalar.activation(gb[h][:, t, :], s_sb[t][:].indirect(n4_sb[:, cols16[h]]), ACT.Copy)
+            nc.scalar.activation(ga[h][:, t, :], s_sb[t][:].indirect(n3_sb[:, cols16[h]]), ACT.Copy)
+            nc.vector.tensor_tensor(pb[h][:, t, :], gb[h][:, t, :], s_sb[t][:, halves[h]], ALU.subtract)
+            nc.vector.tensor_tensor(pa[h][:, t, :], s_sb[t][:, halves[h]], ga[h][:, t, :], ALU.subtract)
+
+        def upper(h, t):
+            nc.vector.scalar_tensor_tensor(up[h][:, t, :], pa[h][:, t, :], 0.0, pb[h][:, t, :], ALU.max, ALU.min)
+
+        def lower(h, t):
+            nc.vector.scalar_tensor_tensor(res[h][:, t, :], pa[h][:, t, :], 0.0, up[h][:, t, :], ALU.min, ALU.max)
+
+        def hand_out(h, engine_copy):
+            nc.sync.dma_start(out_rows[:, :, halves[h]], res[h][:])
+            engine_copy(ri[h][:], res[h][:].rearrange("p t j -> p j t"))
+            nc.vector.quantize_mx(out=rw[h][:].bitcast(FP8X4), scales=rs[:, halves[h]], in_=ri[h][:].rearrange("p j t -> p (j t)"))
+            nc.sync.dma_start(out_words[:, halves[h]], rw[h][:].bitcast(I32))
+
+        fetch_s(*steps[0])
+        for i in range(1, len(steps)):
+            upper(*steps[i - 1])
+            fetch_s(*steps[i])
+            lower(*steps[i - 1])
+        upper(*steps[-1])
+        hand_out(0, nc.scalar.copy)
+        lower(*steps[-1])
+        hand_out(1, nc.vector.tensor_copy)
+        for q in range(4):
+            queue = nc.scalar if q % 2 else nc.sync
+            queue.dma_start(out_2[0, 4 * q : 4 * q + 4, :].bitcast(I32), rs[32 * q : 32 * q + 4, :].bitcast(I32))

@@ -35,6 +35,7 @@ def tile_picked_twcjointbminmod_none_po_kernel(tc, x_words, x_scales, w1_words, 
             for q, queue in enumerate(queues):
                 queue.dma_start(dst[32 * q : 32 * q + 4, :].bitcast(I32), src[0, 4 * q : 4 * q + 4, :].bitcast(I32))
 
+        shared = ctx.enter_context(tc.tile_pool(name="shared", bufs=1))
         xs = sb.tile([P, T], U8, name="xs", align_bytes=64)
         w2s_raw = sb.tile([P, H], U8, name="w2s_raw", align_bytes=64)
         w1s_raw = sb.tile([P, H], U8, name="w1s_raw", align_bytes=64)
@@ -47,15 +48,15 @@ def tile_picked_twcjointbminmod_none_po_kernel(tc, x_words, x_scales, w1_words, 
         w1w_raw = sb.tile([P, 2 * H], U8, name="w1w_raw", align_bytes=64)
         gs_sb = sb.tile([P, PACK], F32, name="gs_sb")
 
-        load_scales([nc.scalar] * 4, xs, x_scales)
         two_sb = load_list(two, "two_sb")
         nc.sync.dma_start(w2w_raw[:].bitcast(I32), w2_words[0].bitcast(I32))
-        cand_sb = load_list(cand, "cand_sb")
-        nc.sync.dma_start(xw[:].bitcast(I32), x_words[0].rearrange("p c r -> p (c r)").bitcast(I32))
-        load_scales([nc.gpsimd, nc.gpsimd, nc.scalar, nc.scalar], w2s_raw, w2_scales)
+        load_scales([nc.sync, nc.scalar, nc.scalar, nc.scalar], w2s_raw, w2_scales)
         n1_sb = load_list(n1, "n1_sb")
+        nc.sync.dma_start(xw[:].bitcast(I32), x_words[0].rearrange("p c r -> p (c r)").bitcast(I32))
+        load_scales([nc.sync] * 4, xs, x_scales)
         n2_sb = load_list(n2, "n2_sb")
         offs_sb = load_list(offs, "offs_sb")
+        cand_sb = load_list(cand, "cand_sb")
         nc.sync.dma_start(w1w_raw[:].bitcast(I32), w1_words[0].bitcast(I32))
         load_scales([nc.sync] * 4, w1s_raw, w1_scales)
         nc.sync.dma_start(gs_sb[:], gs.rearrange("(p t) o -> p (t o)", t=PACK))
@@ -78,19 +79,17 @@ def tile_picked_twcjointbminmod_none_po_kernel(tc, x_words, x_scales, w1_words, 
             )
             return dst
 
-        def pick(table, lst, dtype, name, pieces=1):
+        def pick(dst, table, lst, pieces=1):
             n = lst.shape[1] * 16
-            dst = sb.tile([P, n], dtype, name=name, align_bytes=64)
             step = n // pieces
             for a in range(0, n, step):
                 nc.vector.tensor_copy(dst[:, a : a + step], table[:].indirect(lst[:, a // 16 : (a + step) // 16]))
             return dst
 
         w2w = deal16(w2w_raw, "w2w")
-        two_s = pick(xs, two_sb, U8, "two_s")
-        cand_s = deal(pick(xs, cand_sb, U8, "cand_s_raw", 2), C, U8, "cand_s", 1)
         w2s = deal(w2s_raw, H, U8, "w2s", 1)
-        two_w = pick(xw, two_sb, U32, "two_w")
+        two_w = pick(sb.tile([P, S], U32, name="two_w", align_bytes=64), xw, two_sb)
+        two_s = pick(sb.tile([P, S], U8, name="two_s", align_bytes=64), xs, two_sb)
 
         def first_product(bank, ww, ws, t, tok_w, tok_s):
             nc.tensor.matmul_mx(
@@ -103,20 +102,20 @@ def tile_picked_twcjointbminmod_none_po_kernel(tc, x_words, x_scales, w1_words, 
                 stop=True,
             )
 
-        d_sb = []
+        rows = [sb.tile([P, 2 * S], F32, name=f"rows{t}") for t in range(PACK)]
+        for t in range(PACK):
+            nc.gpsimd.memset(rows[t][:, S:], 0.0)
+
         for t in range(PACK):
             bank = ps.tile([P, S], F32, name=f"d_ps{t}", tag=f"row{t}")
             first_product(bank[:], w2w, w2s, t, two_w, two_s)
-            d_t = sb.tile([P, S], F32, name=f"d{t}")
             if t == 0:
-                nc.scalar.activation(d_t[:], bank[:], ACT.Copy)
+                nc.scalar.activation(rows[t][:, :S], bank[:], ACT.Copy)
             else:
-                nc.vector.tensor_copy(d_t[:], bank[:])
-            d_sb.append(d_t)
+                nc.vector.tensor_copy(rows[t][:, :S], bank[:])
 
-        cand_w = deal(pick(xw, cand_sb, U32, "cand_w_raw", 2), C, U32, "cand_w", 1)
-        offs_s = pick(xs, offs_sb, U8, "offs_s")
-        offs_w = pick(xw, offs_sb, U32, "offs_w")
+        offs_s = pick(sb.tile([P, S], U8, name="offs_s", align_bytes=64), xs, offs_sb)
+        offs_w = pick(sb.tile([P, S], U32, name="offs_w", align_bytes=64), xw, offs_sb)
         w1w = deal16(w1w_raw, "w1w")
         w1s = deal(w1s_raw, H, U8, "w1s", 1)
         y_ps = [ps.tile([P, 2, S], F32, name=f"y_ps{u}") for u in range(2)]
@@ -124,107 +123,108 @@ def tile_picked_twcjointbminmod_none_po_kernel(tc, x_words, x_scales, w1_words, 
             first_product(y_ps[t // 2][:, t % 2, :], w1w, w1s, t, offs_w, offs_s)
 
         halves = [slice(h * HALF, (h + 1) * HALF) for h in range(S // HALF)]
-        cols16 = [slice(h * HALF // 16, (h + 1) * HALF // 16) for h in range(S // HALF)]
+        whole = slice(0, S)
+        last = PACK - 1
+        pieces = [(t, whole) for t in range(last)] + [(last, c) for c in halves]
 
-        g1 = [sb.tile([P, PACK, HALF], F32, name=f"g1_{h}") for h in range(2)]
-        g2 = [sb.tile([P, PACK, HALF], F32, name=f"g2_{h}") for h in range(2)]
-        df = [sb.tile([P, PACK, HALF], F32, name=f"df_{h}") for h in range(2)]
-        th = [sb.tile([P, PACK, HALF], F32, name=f"th_{h}") for h in range(2)]
-        zb = [sb.tile([P, PACK, HALF], BF16, name=f"zb_{h}", align_bytes=64) for h in range(2)]
-        zi = [sb.tile([P, HALF, PACK], BF16, name=f"zi_{h}", align_bytes=64) for h in range(2)]
-        zw = [sb.tile([P, HALF], U32, name=f"zw_{h}", align_bytes=64) for h in range(2)]
-        zs = [sb.tile([P, HALF], U8, name=f"zs_{h}", align_bytes=64) for h in range(2)]
+        def entries(lst, c):
+            return lst[:, c.start // 16 : c.stop // 16]
 
-        def fetch_d(h, t):
-            nc.scalar.activation(g1[h][:, t, :], d_sb[t][:].indirect(n1_sb[:, cols16[h]]), ACT.Copy)
-            nc.scalar.activation(g2[h][:, t, :], d_sb[t][:].indirect(n2_sb[:, cols16[h]]), ACT.Copy)
-            nc.vector.tensor_tensor(df[h][:, t, :], g1[h][:, t, :], g2[h][:, t, :], ALU.subtract)
+        def plane(name, dtype=F32):
+            return sb.tile([P, PACK, S], dtype, name=name, align_bytes=64)
 
-        def gate(h, t):
-            nc.scalar.activation(th[h][:, t, :], df[h][:, t, :], ACT.Tanh)
-            nc.vector.scalar_tensor_tensor(
-                zb[h][:, t, :], y_ps[t // 2][:, t % 2, halves[h]], gs_sb[:, t : t + 1], th[h][:, t, :], ALU.mult, ALU.mult
-            )
+        g1, df = {}, {}
+        cand_w = sb.tile([P, C], U32, name="cand_w", align_bytes=64)
+        cand_dealt = cand_w[:].rearrange("p (t m) -> p m t", t=PACK)
+        for a in range(0, C, S):
+            nc.vector.tensor_copy(cand_dealt[:, a // PACK : (a + S) // PACK, :], xw[:].indirect(cand_sb[:, a // 16 : (a + S) // 16]))
+        cand_s = deal(pick(shared.tile([P, C], U8, name="cand_s_raw", align_bytes=64, offset=1024), xs, cand_sb, 2), C, U8, "cand_s", 1)
+        g2, th = plane("g2"), plane("th")
+        zb = shared.tile([P, PACK, S], BF16, name="zb", align_bytes=64, offset=1280)
+        zi = sb.tile([P, S, PACK], BF16, name="zi", align_bytes=64)
+        zw = sb.tile([P, S], U32, name="zw", align_bytes=64)
+        zs = sb.tile([P, S], U8, name="zs", align_bytes=64)
 
-        def quantise_z(h):
-            nc.vector.tensor_copy(zi[h][:], zb[h][:].rearrange("p t j -> p j t"))
-            nc.vector.quantize_mx(out=zw[h][:].bitcast(FP8X4), scales=zs[h][:], in_=zi[h][:].rearrange("p j t -> p (j t)"))
+        def fetch_d(t, c):
+            g1[t] = sb.tile([P, S], F32, name=f"g1_{t}", align_bytes=64)
+            nc.scalar.activation(g1[t][:, c], rows[t][:].indirect(entries(n1_sb, c)), ACT.Copy)
+            nc.scalar.activation(g2[:, t, c], rows[t][:].indirect(entries(n2_sb, c)), ACT.Copy)
 
-        steps = [(h, t) for h in range(2) for t in range(PACK)]
-        fetch_d(*steps[0])
+        def differ(t, c):
+            if t == last:
+                df[t] = shared.tile([P, S], F32, name=f"df_{t}", align_bytes=64, offset=256)
+            else:
+                df[t] = sb.tile([P, S], F32, name=f"df_{t}", align_bytes=64)
+            engine = nc.vector if t == last else nc.gpsimd
+            engine.tensor_tensor(df[t][:, c], g1[t][:, c], g2[:, t, c], ALU.subtract)
 
-        s_sb = [sb.tile([P, S], F32, name=f"s{t}") for t in range(PACK)]
-        s_first = ps.tile([P, PACK, HALF], F32, name="s_first")
+        def gate(t, c):
+            nc.scalar.activation(th[:, t, c], df[t][:, c], ACT.Tanh)
+            nc.vector.scalar_tensor_tensor(zb[:, t, c], y_ps[t // 2][:, t % 2, c], gs_sb[:, t : t + 1], th[:, t, c], ALU.mult, ALU.mult)
 
-        def score(h):
-            for t in range(PACK):
-                bank = s_first[:, t, :] if h == 0 else ps.tile([P, S], F32, name=f"s_ps{t}", tag=f"row{t}")[:, 0:HALF]
-                nc.tensor.matmul_mx(
-                    out=bank,
-                    lhsT=cand_w[:, P * t : P * (t + 1)].bitcast(FP8X4),
-                    lhsT_scale=cand_s[:, P * t : P * (t + 1)],
-                    rhs=zw[h][:].bitcast(FP8X4),
-                    rhs_scale=zs[h][:],
-                    start=True,
-                    stop=True,
-                )
-                if h == 1:
-                    if t == 0:
-                        nc.scalar.activation(s_sb[t][:, halves[h]], bank, ACT.Copy, scale=0.0625)
-                    else:
-                        nc.vector.tensor_scalar_mul(s_sb[t][:, halves[h]], bank, 0.0625)
-
-        for i in range(1, len(steps)):
-            fetch_d(*steps[i])
-            gate(*steps[i - 1])
-            if steps[i - 1] == (0, PACK - 1):
-                quantise_z(0)
-                score(0)
-        gate(*steps[-1])
-        quantise_z(1)
         for t in range(PACK):
-            nc.scalar.activation(s_sb[t][:, halves[0]], s_first[:, t, :], ACT.Copy, scale=0.0625)
-        score(1)
+            fetch_d(t, whole)
+            differ(t, whole)
+            if t > 0:
+                gate(t - 1, whole)
+        for c in halves:
+            gate(last, c)
 
-        ga = [sb.tile([P, PACK, HALF], F32, name=f"ga_{h}") for h in range(2)]
-        gb = [sb.tile([P, PACK, HALF], F32, name=f"gb_{h}") for h in range(2)]
-        pa = [sb.tile([P, PACK, HALF], F32, name=f"pa_{h}") for h in range(2)]
-        pb = [sb.tile([P, PACK, HALF], F32, name=f"pb_{h}") for h in range(2)]
-        up = [sb.tile([P, PACK, HALF], F32, name=f"up_{h}") for h in range(2)]
-        res = [sb.tile([P, PACK, HALF], F32, name=f"res_{h}") for h in range(2)]
+        nc.scalar.copy(zi[:, halves[0], :], zb[:, :, halves[0]].rearrange("p t j -> p j t"))
+        nc.vector.tensor_copy(zi[:, halves[1], :], zb[:, :, halves[1]].rearrange("p t j -> p j t"))
+        nc.vector.quantize_mx(out=zw[:].bitcast(FP8X4), scales=zs[:], in_=zi[:].rearrange("p j t -> p (j t)"))
+        for t in range(PACK):
+            bank = ps.tile([P, S], F32, name=f"s_ps{t}", tag=f"row{t}")
+            nc.tensor.matmul_mx(
+                out=bank[:],
+                lhsT=cand_w[:, P * t : P * (t + 1)].bitcast(FP8X4),
+                lhsT_scale=cand_s[:, P * t : P * (t + 1)],
+                rhs=zw[:].bitcast(FP8X4),
+                rhs_scale=zs[:],
+                start=True,
+                stop=True,
+            )
+            if t == 0:
+                nc.scalar.activation(rows[t][:, :S], bank[:], ACT.Copy, scale=0.0625)
+            else:
+                nc.vector.tensor_scalar_mul(rows[t][:, :S], bank[:], 0.0625)
+
+        ga, gb, pa, pb, up, res = plane("ga"), plane("gb"), plane("pa"), plane("pb"), plane("up"), plane("res")
         ri = [sb.tile([P, HALF, PACK], BF16, name=f"ri_{h}", align_bytes=64) for h in range(2)]
-        rw = [sb.tile([P, HALF], U32, name=f"rw_{h}", align_bytes=64) for h in range(2)]
+        rw = sb.tile([P, S], U32, name="rw", align_bytes=64)
         rs = sb.tile([P, S], U8, name="rs", align_bytes=64)
         out_rows = out_0.rearrange("(p t) j -> p t j", t=PACK)
         out_words = out_1[0].rearrange("p c r -> p (c r)").bitcast(I32)
 
-        def fetch_s(h, t):
-            nc.scalar.activation(gb[h][:, t, :], s_sb[t][:].indirect(n4_sb[:, cols16[h]]), ACT.Copy)
-            nc.scalar.activation(ga[h][:, t, :], s_sb[t][:].indirect(n3_sb[:, cols16[h]]), ACT.Copy)
-            nc.vector.tensor_tensor(pb[h][:, t, :], gb[h][:, t, :], s_sb[t][:, halves[h]], ALU.subtract)
-            nc.vector.tensor_tensor(pa[h][:, t, :], s_sb[t][:, halves[h]], ga[h][:, t, :], ALU.subtract)
+        def fetch_s(t, c):
+            nc.scalar.activation(gb[:, t, c], rows[t][:].indirect(entries(n4_sb, c)), ACT.Copy)
+            nc.scalar.activation(ga[:, t, c], rows[t][:].indirect(entries(n3_sb, c)), ACT.Copy)
+            nc.vector.tensor_tensor(pb[:, t, c], gb[:, t, c], rows[t][:, c], ALU.subtract)
+            nc.vector.tensor_tensor(pa[:, t, c], rows[t][:, c], ga[:, t, c], ALU.subtract)
 
-        def upper(h, t):
-            nc.vector.scalar_tensor_tensor(up[h][:, t, :], pa[h][:, t, :], 0.0, pb[h][:, t, :], ALU.max, ALU.min)
+        def upper(t, c):
+            nc.vector.scalar_tensor_tensor(up[:, t, c], pa[:, t, c], 0.0, pb[:, t, c], ALU.max, ALU.min)
 
-        def lower(h, t):
-            nc.vector.scalar_tensor_tensor(res[h][:, t, :], pa[h][:, t, :], 0.0, up[h][:, t, :], ALU.min, ALU.max)
+        def lower(t, c):
+            nc.vector.scalar_tensor_tensor(res[:, t, c], pa[:, t, c], 0.0, up[:, t, c], ALU.min, ALU.max)
 
         def hand_out(h, engine_copy):
-            nc.sync.dma_start(out_rows[:, :, halves[h]], res[h][:])
-            engine_copy(ri[h][:], res[h][:].rearrange("p t j -> p j t"))
-            nc.vector.quantize_mx(out=rw[h][:].bitcast(FP8X4), scales=rs[:, halves[h]], in_=ri[h][:].rearrange("p j t -> p (j t)"))
-            nc.sync.dma_start(out_words[:, halves[h]], rw[h][:].bitcast(I32))
+            engine_copy(ri[h][:], res[:, :, halves[h]].rearrange("p t j -> p j t"))
+            nc.vector.quantize_mx(out=rw[:, halves[h]].bitcast(FP8X4), scales=rs[:, halves[h]], in_=ri[h][:].rearrange("p j t -> p (j t)"))
 
-        fetch_s(*steps[0])
-        for i in range(1, len(steps)):
-            upper(*steps[i - 1])
-            fetch_s(*steps[i])
-            lower(*steps[i - 1])
-        upper(*steps[-1])
+        fetch_s(*pieces[0])
+        for i in range(1, len(pieces)):
+            upper(*pieces[i - 1])
+            fetch_s(*pieces[i])
+            lower(*pieces[i - 1])
+            if i == len(pieces) - 2:
+                nc.sync.dma_start(out_rows[:, :last, :], res[:, :last, :])
+        upper(*pieces[-1])
         hand_out(0, nc.scalar.copy)
-        lower(*steps[-1])
+        lower(*pieces[-1])
+        nc.sync.dma_start(out_rows[:, last, :], res[:, last, :])
         hand_out(1, nc.vector.tensor_copy)
+        nc.sync.dma_start(out_words, rw[:].bitcast(I32))
         for q in range(4):
-            queue = nc.scalar if q % 2 else nc.sync
+            queue = nc.scalar if q % 2 == 0 else nc.sync
             queue.dma_start(out_2[0, 4 * q : 4 * q + 4, :].bitcast(I32), rs[32 * q : 32 * q + 4, :].bitcast(I32))

@@ -38,14 +38,14 @@ def tile_picked_twcjointbminmod_none_po_kernel(tc, x_words, x_scales, w1_words, 
         shared = ctx.enter_context(tc.tile_pool(name="shared", bufs=1))
         xs = sb.tile([P, T], U8, name="xs", align_bytes=64)
         w2s_raw = sb.tile([P, H], U8, name="w2s_raw", align_bytes=64)
-        w1s_raw = sb.tile([P, H], U8, name="w1s_raw", align_bytes=64)
+        w1s_raw = shared.tile([P, H], U8, name="w1s_raw", align_bytes=64, offset=C)
         nc.vector.memset(xs[:].bitcast(I32), 0)
         nc.gpsimd.memset(w2s_raw[:].bitcast(I32), 0)
         nc.vector.memset(w1s_raw[:].bitcast(I32), 0)
 
         xw = sb.tile([P, T], U32, name="xw", align_bytes=64)
         w2w_raw = sb.tile([P, 2 * H], U8, name="w2w_raw", align_bytes=64)
-        w1w_raw = sb.tile([P, 2 * H], U8, name="w1w_raw", align_bytes=64)
+        w1w_raw = shared.tile([P, 2 * H], U8, name="w1w_raw", align_bytes=64, offset=C + H)
         gs_sb = sb.tile([P, PACK], F32, name="gs_sb")
 
         two_sb = load_list(two, "two_sb")
@@ -102,14 +102,14 @@ def tile_picked_twcjointbminmod_none_po_kernel(tc, x_words, x_scales, w1_words, 
                 stop=True,
             )
 
-        rows = [sb.tile([P, 2 * S], F32, name=f"rows{t}") for t in range(PACK)]
+        rows = [sb.tile([P, 2 * S], F32, name=f"rows{t}", tag=f"rows{t}", align_bytes=64) for t in range(PACK)]
         for t in range(PACK):
             nc.gpsimd.memset(rows[t][:, S:], 0.0)
 
         for t in range(PACK):
             bank = ps.tile([P, S], F32, name=f"d_ps{t}", tag=f"row{t}")
             first_product(bank[:], w2w, w2s, t, two_w, two_s)
-            if t == 0:
+            if t < PACK - 1:
                 nc.scalar.activation(rows[t][:, :S], bank[:], ACT.Copy)
             else:
                 nc.vector.tensor_copy(rows[t][:, :S], bank[:])
@@ -133,42 +133,32 @@ def tile_picked_twcjointbminmod_none_po_kernel(tc, x_words, x_scales, w1_words, 
         def plane(name, dtype=F32):
             return sb.tile([P, PACK, S], dtype, name=name, align_bytes=64)
 
-        g1, df = {}, {}
         cand_w = sb.tile([P, C], U32, name="cand_w", align_bytes=64)
         cand_dealt = cand_w[:].rearrange("p (t m) -> p m t", t=PACK)
         for a in range(0, C, S):
             nc.vector.tensor_copy(cand_dealt[:, a // PACK : (a + S) // PACK, :], xw[:].indirect(cand_sb[:, a // 16 : (a + S) // 16]))
-        cand_s = deal(pick(shared.tile([P, C], U8, name="cand_s_raw", align_bytes=64, offset=1024), xs, cand_sb, 2), C, U8, "cand_s", 1)
-        g2, th = plane("g2"), plane("th")
-        zb = shared.tile([P, PACK, S], BF16, name="zb", align_bytes=64, offset=1280)
+        cand_s = deal(pick(shared.tile([P, C], U8, name="cand_s_raw", align_bytes=64, offset=0), xs, cand_sb, 2), C, U8, "cand_s", 1)
+        g1, g2, zb = plane("g1"), plane("g2"), plane("zb", BF16)
+        df = shared.tile([P, PACK, S], F32, name="df", align_bytes=64, offset=0)
         zi = sb.tile([P, S, PACK], BF16, name="zi", align_bytes=64)
         zw = sb.tile([P, S], U32, name="zw", align_bytes=64)
         zs = sb.tile([P, S], U8, name="zs", align_bytes=64)
 
         def fetch_d(t, c):
-            g1[t] = sb.tile([P, S], F32, name=f"g1_{t}", align_bytes=64)
-            nc.scalar.activation(g1[t][:, c], rows[t][:].indirect(entries(n1_sb, c)), ACT.Copy)
+            nc.scalar.activation(g1[:, t, c], rows[t][:].indirect(entries(n1_sb, c)), ACT.Copy)
             nc.scalar.activation(g2[:, t, c], rows[t][:].indirect(entries(n2_sb, c)), ACT.Copy)
 
-        def differ(t, c):
-            if t == last:
-                df[t] = shared.tile([P, S], F32, name=f"df_{t}", align_bytes=64, offset=256)
-            else:
-                df[t] = sb.tile([P, S], F32, name=f"df_{t}", align_bytes=64)
-            engine = nc.vector if t == last else nc.gpsimd
-            engine.tensor_tensor(df[t][:, c], g1[t][:, c], g2[:, t, c], ALU.subtract)
-
         def gate(t, c):
-            nc.scalar.activation(th[:, t, c], df[t][:, c], ACT.Tanh)
+            nc.scalar.activation(th[:, t, c], df[:, t, c], ACT.Tanh)
             nc.vector.scalar_tensor_tensor(zb[:, t, c], y_ps[t // 2][:, t % 2, c], gs_sb[:, t : t + 1], th[:, t, c], ALU.mult, ALU.mult)
 
         for t in range(PACK):
             fetch_d(t, whole)
-            differ(t, whole)
-            if t > 0:
-                gate(t - 1, whole)
-        for c in halves:
-            gate(last, c)
+            nc.vector.tensor_tensor(df[:, t, :], g1[:, t, :], g2[:, t, :], ALU.subtract)
+        th = sb.tile([P, PACK, S], F32, name="th", tag=f"rows{last}", align_bytes=64)
+        for piece in pieces:
+            gate(*piece)
+        rows[last] = sb.tile([P, S], F32, name="s_last", align_bytes=64)
 
         nc.scalar.copy(zi[:, halves[0], :], zb[:, :, halves[0]].rearrange("p t j -> p j t"))
         nc.vector.tensor_copy(zi[:, halves[1], :], zb[:, :, halves[1]].rearrange("p t j -> p j t"))

@@ -16,26 +16,32 @@ ALU = mybir.AluOpType
 P = 128
 K, T, S, H, C = 512, 2048, 256, 512, 512
 PACK = 4
-HALF = 128
+GROUP = 16
+QUADRANT = 32
+HALF = S // 2
+SCORE_SCALE = 0.0625
 FLOPS = 2 * K * (H * S + H * S + C * S)
 
 
-def tile_picked_twcjointbminmod_none_po_kernel(tc, x_words, x_scales, w1_words, w1_scales, w2_words, w2_scales, gs, offs, two, n1, n2, cand, n3, n4, out_0, out_1, out_2):
+def tile_picked_twcjointbminmod_none_po_kernel(
+    tc, x_words, x_scales, w1_words, w1_scales, w2_words, w2_scales, gs, offs, two, n1, n2, cand, n3, n4, out_0, out_1, out_2
+):
     nc = tc.nc
     with ExitStack() as ctx:
         sb = ctx.enter_context(tc.tile_pool(name="sb", bufs=1))
         ps = ctx.enter_context(tc.psum_pool(name="ps", bufs=1))
 
         def load_list(src, name):
-            t = sb.tile([P, src.shape[1]], U16, name=name)
-            nc.sync.dma_start(t[:], src)
-            return t
+            lst = sb.tile([P, src.shape[1]], U16, name=name)
+            nc.sync.dma_start(lst[:], src)
+            return lst
 
         def load_scales(queues, dst, src):
             for q, queue in enumerate(queues):
-                queue.dma_start(dst[32 * q : 32 * q + 4, :].bitcast(I32), src[0, 4 * q : 4 * q + 4, :].bitcast(I32))
+                queue.dma_start(dst[QUADRANT * q : QUADRANT * q + 4, :].bitcast(I32), src[0, 4 * q : 4 * q + 4, :].bitcast(I32))
 
         shared = ctx.enter_context(tc.tile_pool(name="shared", bufs=1))
+
         xs = sb.tile([P, T], U8, name="xs", align_bytes=64)
         w2s_raw = sb.tile([P, H], U8, name="w2s_raw", align_bytes=64)
         w1s_raw = shared.tile([P, H], U8, name="w1s_raw", align_bytes=64, offset=C)
@@ -63,15 +69,15 @@ def tile_picked_twcjointbminmod_none_po_kernel(tc, x_words, x_scales, w1_words, 
         n4_sb = load_list(n4, "n4_sb")
         n3_sb = load_list(n3, "n3_sb")
 
-        def deal(src, width, dtype, name, per):
-            dst = sb.tile([P, width * per], dtype, name=name, align_bytes=64)
+        def deal_scales(src, name):
+            dst = sb.tile([P, PACK * P], U8, name=name, align_bytes=64)
             nc.vector.tensor_copy(
-                dst[:].rearrange("p (t m b) -> p t m b", t=PACK, b=per),
-                src[:].rearrange("p (m t b) -> p t m b", t=PACK, b=per),
+                dst[:].rearrange("p (t m) -> p t m", t=PACK),
+                src[:].rearrange("p (m t) -> p t m", t=PACK),
             )
             return dst
 
-        def deal16(src, name):
+        def deal_words(src, name):
             dst = sb.tile([P, 2 * H], U8, name=name, align_bytes=64)
             nc.vector.tensor_copy(
                 dst[:].bitcast(U16).rearrange("p (t m) -> p t m", t=PACK),
@@ -79,90 +85,89 @@ def tile_picked_twcjointbminmod_none_po_kernel(tc, x_words, x_scales, w1_words, 
             )
             return dst
 
-        def pick(dst, table, lst, pieces=1):
-            n = lst.shape[1] * 16
-            step = n // pieces
-            for a in range(0, n, step):
-                nc.vector.tensor_copy(dst[:, a : a + step], table[:].indirect(lst[:, a // 16 : (a + step) // 16]))
+        def entries(lst, cols):
+            return lst[:, cols.start // GROUP : cols.stop // GROUP]
+
+        def pick(dst, table, lst):
+            nc.vector.tensor_copy(dst[:], table[:].indirect(lst[:]))
             return dst
 
-        w2w = deal16(w2w_raw, "w2w")
-        w2s = deal(w2s_raw, H, U8, "w2s", 1)
-        two_w = pick(sb.tile([P, S], U32, name="two_w", align_bytes=64), xw, two_sb)
-        two_s = pick(sb.tile([P, S], U8, name="two_s", align_bytes=64), xs, two_sb)
-
-        def first_product(bank, ww, ws, t, tok_w, tok_s):
+        def project(bank, w_words, w_scales, t, tok_words, tok_scales):
             nc.tensor.matmul_mx(
                 out=bank,
-                lhsT=ww[:, 2 * P * t : 2 * P * (t + 1)].bitcast(FP4X4),
-                lhsT_scale=ws[:, P * t : P * (t + 1)],
-                rhs=tok_w[:].bitcast(FP8X4),
-                rhs_scale=tok_s[:],
+                lhsT=w_words[:, 2 * P * t : 2 * P * (t + 1)].bitcast(FP4X4),
+                lhsT_scale=w_scales[:, P * t : P * (t + 1)],
+                rhs=tok_words[:].bitcast(FP8X4),
+                rhs_scale=tok_scales[:],
                 start=True,
                 stop=True,
             )
 
+        w2w = deal_words(w2w_raw, "w2w")
+        w2s = deal_scales(w2s_raw, "w2s")
+        two_w = pick(sb.tile([P, S], U32, name="two_w", align_bytes=64), xw, two_sb)
+        two_s = pick(sb.tile([P, S], U8, name="two_s", align_bytes=64), xs, two_sb)
+
+        last = PACK - 1
         rows = [sb.tile([P, 2 * S], F32, name=f"rows{t}", tag=f"rows{t}", align_bytes=64) for t in range(PACK)]
         for t in range(PACK):
             nc.gpsimd.memset(rows[t][:, S:], 0.0)
 
         for t in range(PACK):
             bank = ps.tile([P, S], F32, name=f"d_ps{t}", tag=f"row{t}")
-            first_product(bank[:], w2w, w2s, t, two_w, two_s)
-            if t < PACK - 1:
+            project(bank[:], w2w, w2s, t, two_w, two_s)
+            if t > 0:
                 nc.scalar.activation(rows[t][:, :S], bank[:], ACT.Copy)
             else:
                 nc.vector.tensor_copy(rows[t][:, :S], bank[:])
 
         offs_s = pick(sb.tile([P, S], U8, name="offs_s", align_bytes=64), xs, offs_sb)
         offs_w = pick(sb.tile([P, S], U32, name="offs_w", align_bytes=64), xw, offs_sb)
-        w1w = deal16(w1w_raw, "w1w")
-        w1s = deal(w1s_raw, H, U8, "w1s", 1)
+        w1w = deal_words(w1w_raw, "w1w")
+        w1s = deal_scales(w1s_raw, "w1s")
         y_ps = [ps.tile([P, 2, S], F32, name=f"y_ps{u}") for u in range(2)]
         for t in range(PACK):
-            first_product(y_ps[t // 2][:, t % 2, :], w1w, w1s, t, offs_w, offs_s)
+            project(y_ps[t // 2][:, t % 2, :], w1w, w1s, t, offs_w, offs_s)
 
-        halves = [slice(h * HALF, (h + 1) * HALF) for h in range(S // HALF)]
+        halves = [slice(0, HALF), slice(HALF, S)]
         whole = slice(0, S)
-        last = PACK - 1
-        pieces = [(t, whole) for t in range(last)] + [(last, c) for c in halves]
+        pieces = [(t, whole) for t in range(last)] + [(last, cols) for cols in halves]
 
-        def entries(lst, c):
-            return lst[:, c.start // 16 : c.stop // 16]
-
-        def plane(name, dtype=F32):
+        def row_tiles(name, dtype=F32):
             return sb.tile([P, PACK, S], dtype, name=name, align_bytes=64)
 
+        def weave(engine_copy, dst, src):
+            engine_copy(dst.rearrange("p (c i) t -> p c t i", i=PACK), src.rearrange("p t (c i) -> p c t i", i=PACK))
+
         cand_w = sb.tile([P, C], U32, name="cand_w", align_bytes=64)
-        cand_dealt = cand_w[:].rearrange("p (t m) -> p m t", t=PACK)
-        for a in range(0, C, S):
-            nc.vector.tensor_copy(cand_dealt[:, a // PACK : (a + S) // PACK, :], xw[:].indirect(cand_sb[:, a // 16 : (a + S) // 16]))
-        cand_s = deal(pick(shared.tile([P, C], U8, name="cand_s_raw", align_bytes=64, offset=0), xs, cand_sb, 2), C, U8, "cand_s", 1)
-        g1, g2, zb = plane("g1"), plane("g2"), plane("zb", BF16)
+        nc.vector.tensor_copy(cand_w[:].rearrange("p (t m) -> p m t", t=PACK), xw[:].indirect(cand_sb[:]))
+        cand_s_raw = shared.tile([P, C], U8, name="cand_s_raw", align_bytes=64, offset=0)
+        cand_s = deal_scales(pick(cand_s_raw, xs, cand_sb), "cand_s")
+
+        g1, g2, zb = row_tiles("g1"), row_tiles("g2"), row_tiles("zb", BF16)
         df = shared.tile([P, PACK, S], F32, name="df", align_bytes=64, offset=0)
         zi = sb.tile([P, S, PACK], BF16, name="zi", align_bytes=64)
         zw = sb.tile([P, S], U32, name="zw", align_bytes=64)
         zs = sb.tile([P, S], U8, name="zs", align_bytes=64)
 
-        def fetch_d(t, c):
-            nc.scalar.activation(g1[:, t, c], rows[t][:].indirect(entries(n1_sb, c)), ACT.Copy)
-            nc.scalar.activation(g2[:, t, c], rows[t][:].indirect(entries(n2_sb, c)), ACT.Copy)
-
-        def gate(t, c):
-            nc.scalar.activation(th[:, t, c], df[:, t, c], ACT.Tanh)
-            nc.vector.scalar_tensor_tensor(zb[:, t, c], y_ps[t // 2][:, t % 2, c], gs_sb[:, t : t + 1], th[:, t, c], ALU.mult, ALU.mult)
-
         for t in range(PACK):
-            fetch_d(t, whole)
+            nc.scalar.activation(g1[:, t, :], rows[t][:].indirect(n1_sb[:]), ACT.Copy)
+            nc.scalar.activation(g2[:, t, :], rows[t][:].indirect(n2_sb[:]), ACT.Copy)
             nc.vector.tensor_tensor(df[:, t, :], g1[:, t, :], g2[:, t, :], ALU.subtract)
+
         th = sb.tile([P, PACK, S], F32, name="th", tag=f"rows{last}", align_bytes=64)
-        for piece in pieces:
-            gate(*piece)
+        for t, cols in pieces:
+            nc.scalar.activation(th[:, t, cols], df[:, t, cols], ACT.Tanh)
+            nc.vector.scalar_tensor_tensor(
+                zb[:, t, cols], y_ps[t // 2][:, t % 2, cols], gs_sb[:, t : t + 1], th[:, t, cols], ALU.mult, ALU.mult
+            )
+
         rows[last] = sb.tile([P, S], F32, name="s_last", align_bytes=64)
 
-        nc.scalar.copy(zi[:, halves[0], :], zb[:, :, halves[0]].rearrange("p t j -> p j t"))
-        nc.vector.tensor_copy(zi[:, halves[1], :], zb[:, :, halves[1]].rearrange("p t j -> p j t"))
+        weave(nc.scalar.copy, zi[:, halves[0], :], zb[:, :, halves[0]])
+        weave(nc.vector.tensor_copy, zi[:, halves[1], :], zb[:, :, halves[1]])
         nc.vector.quantize_mx(out=zw[:].bitcast(FP8X4), scales=zs[:], in_=zi[:].rearrange("p j t -> p (j t)"))
+
         for t in range(PACK):
             bank = ps.tile([P, S], F32, name=f"s_ps{t}", tag=f"row{t}")
             nc.tensor.matmul_mx(
@@ -175,46 +180,46 @@ def tile_picked_twcjointbminmod_none_po_kernel(tc, x_words, x_scales, w1_words, 
                 stop=True,
             )
             if t == 0:
-                nc.scalar.activation(rows[t][:, :S], bank[:], ACT.Copy, scale=0.0625)
+                nc.scalar.activation(rows[t][:, :S], bank[:], ACT.Copy, scale=SCORE_SCALE)
             else:
-                nc.vector.tensor_scalar_mul(rows[t][:, :S], bank[:], 0.0625)
+                nc.vector.tensor_scalar_mul(rows[t][:, :S], bank[:], SCORE_SCALE)
 
-        ga, gb, pa, pb, up, res = plane("ga"), plane("gb"), plane("pa"), plane("pb"), plane("up"), plane("res")
+        ga, gb, pa, pb, up, res = [row_tiles(name) for name in ("ga", "gb", "pa", "pb", "up", "res")]
         ri = [sb.tile([P, HALF, PACK], BF16, name=f"ri_{h}", align_bytes=64) for h in range(2)]
         rw = sb.tile([P, S], U32, name="rw", align_bytes=64)
         rs = sb.tile([P, S], U8, name="rs", align_bytes=64)
         out_rows = out_0.rearrange("(p t) j -> p t j", t=PACK)
         out_words = out_1[0].rearrange("p c r -> p (c r)").bitcast(I32)
 
-        def fetch_s(t, c):
-            nc.scalar.activation(gb[:, t, c], rows[t][:].indirect(entries(n4_sb, c)), ACT.Copy)
-            nc.scalar.activation(ga[:, t, c], rows[t][:].indirect(entries(n3_sb, c)), ACT.Copy)
-            nc.vector.tensor_tensor(pb[:, t, c], gb[:, t, c], rows[t][:, c], ALU.subtract)
-            nc.vector.tensor_tensor(pa[:, t, c], rows[t][:, c], ga[:, t, c], ALU.subtract)
+        def differences(t, cols):
+            nc.scalar.activation(gb[:, t, cols], rows[t][:].indirect(entries(n4_sb, cols)), ACT.Copy)
+            nc.scalar.activation(ga[:, t, cols], rows[t][:].indirect(entries(n3_sb, cols)), ACT.Copy)
+            nc.vector.tensor_tensor(pb[:, t, cols], gb[:, t, cols], rows[t][:, cols], ALU.subtract)
+            nc.vector.tensor_tensor(pa[:, t, cols], rows[t][:, cols], ga[:, t, cols], ALU.subtract)
 
-        def upper(t, c):
-            nc.vector.scalar_tensor_tensor(up[:, t, c], pa[:, t, c], 0.0, pb[:, t, c], ALU.max, ALU.min)
+        def clamp_above(t, cols):
+            nc.vector.scalar_tensor_tensor(up[:, t, cols], pa[:, t, cols], 0.0, pb[:, t, cols], ALU.max, ALU.min)
 
-        def lower(t, c):
-            nc.vector.scalar_tensor_tensor(res[:, t, c], pa[:, t, c], 0.0, up[:, t, c], ALU.min, ALU.max)
+        def clamp_below(t, cols):
+            nc.vector.scalar_tensor_tensor(res[:, t, cols], pa[:, t, cols], 0.0, up[:, t, cols], ALU.min, ALU.max)
 
-        def hand_out(h, engine_copy):
-            engine_copy(ri[h][:], res[:, :, halves[h]].rearrange("p t j -> p j t"))
+        def quantise_result(h, engine_copy):
+            weave(engine_copy, ri[h][:], res[:, :, halves[h]])
             nc.vector.quantize_mx(out=rw[:, halves[h]].bitcast(FP8X4), scales=rs[:, halves[h]], in_=ri[h][:].rearrange("p j t -> p (j t)"))
 
-        fetch_s(*pieces[0])
-        for i in range(1, len(pieces)):
-            upper(*pieces[i - 1])
-            fetch_s(*pieces[i])
-            lower(*pieces[i - 1])
-            if i == len(pieces) - 2:
+        differences(*pieces[0])
+        for before, piece in zip(pieces, pieces[1:]):
+            clamp_above(*before)
+            differences(*piece)
+            clamp_below(*before)
+            if before[0] == last - 1:
                 nc.sync.dma_start(out_rows[:, :last, :], res[:, :last, :])
-        upper(*pieces[-1])
-        hand_out(0, nc.scalar.copy)
-        lower(*pieces[-1])
+        clamp_above(*pieces[-1])
+        quantise_result(0, nc.scalar.copy)
+        clamp_below(*pieces[-1])
         nc.sync.dma_start(out_rows[:, last, :], res[:, last, :])
-        hand_out(1, nc.vector.tensor_copy)
+        quantise_result(1, nc.vector.tensor_copy)
         nc.sync.dma_start(out_words, rw[:].bitcast(I32))
-        for q in range(4):
+        for q in range(P // QUADRANT):
             queue = nc.scalar if q % 2 == 0 else nc.sync
-            queue.dma_start(out_2[0, 4 * q : 4 * q + 4, :].bitcast(I32), rs[32 * q : 32 * q + 4, :].bitcast(I32))
+            queue.dma_start(out_2[0, 4 * q : 4 * q + 4, :].bitcast(I32), rs[QUADRANT * q : QUADRANT * q + 4, :].bitcast(I32))

from contextlib import ExitStack

import concourse.mybir as mybir

F32 = mybir.dt.float32
BF16 = mybir.dt.bfloat16
I32 = mybir.dt.int32
U32 = mybir.dt.uint32
U16 = mybir.dt.uint16
U8 = mybir.dt.uint8
FP8X4 = mybir.dt.float8_e4m3fn_x4
FP4X4 = mybir.dt.float4_e2m1fn_x4
ACT = mybir.ActivationFunctionType
ALU = mybir.AluOpType

P = 128
K, T, S, H, C = 512, 2048, 256, 512, 512
PACK = 4
GROUP = 16
QUADRANT = 32
HALF = S // 2
SCORE_SCALE = 0.0625
FLOPS = 2 * K * (H * S + H * S + C * S)


def tile_picked_twcjointbminmod_none_po_kernel(
    tc, x_words, x_scales, w1_words, w1_scales, w2_words, w2_scales, gs, offs, two, n1, n2, cand, n3, n4, out_0, out_1, out_2
):
    nc = tc.nc
    with ExitStack() as ctx:
        sb = ctx.enter_context(tc.tile_pool(name="sb", bufs=1))
        ps = ctx.enter_context(tc.psum_pool(name="ps", bufs=1))

        def load_list(src, name):
            lst = sb.tile([P, src.shape[1]], U16, name=name)
            nc.sync.dma_start(lst[:], src)
            return lst

        def load_scales(queues, dst, src):
            for q, queue in enumerate(queues):
                queue.dma_start(dst[QUADRANT * q : QUADRANT * q + 4, :].bitcast(I32), src[0, 4 * q : 4 * q + 4, :].bitcast(I32))

        shared = ctx.enter_context(tc.tile_pool(name="shared", bufs=1))

        xs = sb.tile([P, T], U8, name="xs", align_bytes=64)
        w2s_raw = sb.tile([P, H], U8, name="w2s_raw", align_bytes=64)
        w1s_raw = shared.tile([P, H], U8, name="w1s_raw", align_bytes=64, offset=C)
        nc.vector.memset(xs[:].bitcast(I32), 0)
        nc.gpsimd.memset(w2s_raw[:].bitcast(I32), 0)
        nc.vector.memset(w1s_raw[:].bitcast(I32), 0)

        xw = sb.tile([P, T], U32, name="xw", align_bytes=64)
        w2w_raw = sb.tile([P, 2 * H], U8, name="w2w_raw", align_bytes=64)
        w1w_raw = shared.tile([P, 2 * H], U8, name="w1w_raw", align_bytes=64, offset=C + H)
        gs_sb = sb.tile([P, PACK], F32, name="gs_sb")

        two_sb = load_list(two, "two_sb")
        nc.sync.dma_start(w2w_raw[:].bitcast(I32), w2_words[0].bitcast(I32))
        load_scales([nc.sync, nc.scalar, nc.scalar, nc.scalar], w2s_raw, w2_scales)
        n1_sb = load_list(n1, "n1_sb")
        nc.sync.dma_start(xw[:].bitcast(I32), x_words[0].rearrange("p c r -> p (c r)").bitcast(I32))
        load_scales([nc.sync] * 4, xs, x_scales)
        n2_sb = load_list(n2, "n2_sb")
        offs_sb = load_list(offs, "offs_sb")
        cand_sb = load_list(cand, "cand_sb")
        nc.sync.dma_start(w1w_raw[:].bitcast(I32), w1_words[0].bitcast(I32))
        load_scales([nc.sync] * 4, w1s_raw, w1_scales)
        nc.sync.dma_start(gs_sb[:], gs.rearrange("(p t) o -> p (t o)", t=PACK))
        n4_sb = load_list(n4, "n4_sb")
        n3_sb = load_list(n3, "n3_sb")

        def deal_scales(src, name):
            dst = sb.tile([P, PACK * P], U8, name=name, align_bytes=64)
            nc.vector.tensor_copy(
                dst[:].rearrange("p (t m) -> p t m", t=PACK),
                src[:].rearrange("p (m t) -> p t m", t=PACK),
            )
            return dst

        def deal_words(src, name):
            dst = sb.tile([P, 2 * H], U8, name=name, align_bytes=64)
            nc.vector.tensor_copy(
                dst[:].bitcast(U16).rearrange("p (t m) -> p t m", t=PACK),
                src[:].bitcast(U16).rearrange("p (m t) -> p t m", t=PACK),
            )
            return dst

        def entries(lst, cols):
            return lst[:, cols.start // GROUP : cols.stop // GROUP]

        def pick(dst, table, lst):
            nc.vector.tensor_copy(dst[:], table[:].indirect(lst[:]))
            return dst

        def project(bank, w_words, w_scales, t, tok_words, tok_scales):
            nc.tensor.matmul_mx(
                out=bank,
                lhsT=w_words[:, 2 * P * t : 2 * P * (t + 1)].bitcast(FP4X4),
                lhsT_scale=w_scales[:, P * t : P * (t + 1)],
                rhs=tok_words[:].bitcast(FP8X4),
                rhs_scale=tok_scales[:],
                start=True,
                stop=True,
            )

        w2w = deal_words(w2w_raw, "w2w")
        w2s = deal_scales(w2s_raw, "w2s")
        two_w = pick(sb.tile([P, S], U32, name="two_w", align_bytes=64), xw, two_sb)
        two_s = pick(sb.tile([P, S], U8, name="two_s", align_bytes=64), xs, two_sb)

        last = PACK - 1
        rows = [sb.tile([P, 2 * S], F32, name=f"rows{t}", tag=f"rows{t}", align_bytes=64) for t in range(PACK)]
        for t in range(PACK):
            nc.gpsimd.memset(rows[t][:, S:], 0.0)

        for t in range(PACK):
            bank = ps.tile([P, S], F32, name=f"d_ps{t}", tag=f"row{t}")
            project(bank[:], w2w, w2s, t, two_w, two_s)
            if t > 0:
                nc.scalar.activation(rows[t][:, :S], bank[:], ACT.Copy)
            else:
                nc.vector.tensor_copy(rows[t][:, :S], bank[:])

        offs_s = pick(sb.tile([P, S], U8, name="offs_s", align_bytes=64), xs, offs_sb)
        offs_w = pick(sb.tile([P, S], U32, name="offs_w", align_bytes=64), xw, offs_sb)
        w1w = deal_words(w1w_raw, "w1w")
        w1s = deal_scales(w1s_raw, "w1s")
        y_ps = [ps.tile([P, 2, S], F32, name=f"y_ps{u}") for u in range(2)]
        for t in range(PACK):
            project(y_ps[t // 2][:, t % 2, :], w1w, w1s, t, offs_w, offs_s)

        halves = [slice(0, HALF), slice(HALF, S)]
        whole = slice(0, S)
        pieces = [(t, whole) for t in range(last)] + [(last, cols) for cols in halves]

        def row_tiles(name, dtype=F32):
            return sb.tile([P, PACK, S], dtype, name=name, align_bytes=64)

        def weave(engine_copy, dst, src):
            engine_copy(dst.rearrange("p (c i) t -> p c t i", i=PACK), src.rearrange("p t (c i) -> p c t i", i=PACK))

        cand_w = sb.tile([P, C], U32, name="cand_w", align_bytes=64)
        nc.vector.tensor_copy(cand_w[:].rearrange("p (t m) -> p m t", t=PACK), xw[:].indirect(cand_sb[:]))
        cand_s_raw = shared.tile([P, C], U8, name="cand_s_raw", align_bytes=64, offset=0)
        cand_s = deal_scales(pick(cand_s_raw, xs, cand_sb), "cand_s")

        g1, g2, zb = row_tiles("g1"), row_tiles("g2"), row_tiles("zb", BF16)
        df = shared.tile([P, PACK, S], F32, name="df", align_bytes=64, offset=0)
        zi = sb.tile([P, S, PACK], BF16, name="zi", align_bytes=64)
        zw = sb.tile([P, S], U32, name="zw", align_bytes=64)
        zs = sb.tile([P, S], U8, name="zs", align_bytes=64)

        for t in range(PACK):
            nc.scalar.activation(g1[:, t, :], rows[t][:].indirect(n1_sb[:]), ACT.Copy)
            nc.scalar.activation(g2[:, t, :], rows[t][:].indirect(n2_sb[:]), ACT.Copy)
            nc.vector.tensor_tensor(df[:, t, :], g1[:, t, :], g2[:, t, :], ALU.subtract)

        th = sb.tile([P, PACK, S], F32, name="th", tag=f"rows{last}", align_bytes=64)
        for t, cols in pieces:
            nc.scalar.activation(th[:, t, cols], df[:, t, cols], ACT.Tanh)
            nc.vector.scalar_tensor_tensor(
                zb[:, t, cols], y_ps[t // 2][:, t % 2, cols], gs_sb[:, t : t + 1], th[:, t, cols], ALU.mult, ALU.mult
            )

        rows[last] = sb.tile([P, S], F32, name="s_last", align_bytes=64)

        weave(nc.scalar.copy, zi[:, halves[0], :], zb[:, :, halves[0]])
        weave(nc.vector.tensor_copy, zi[:, halves[1], :], zb[:, :, halves[1]])
        nc.vector.quantize_mx(out=zw[:].bitcast(FP8X4), scales=zs[:], in_=zi[:].rearrange("p j t -> p (j t)"))

        for t in range(PACK):
            bank = ps.tile([P, S], F32, name=f"s_ps{t}", tag=f"row{t}")
            nc.tensor.matmul_mx(
                out=bank[:],
                lhsT=cand_w[:, P * t : P * (t + 1)].bitcast(FP8X4),
                lhsT_scale=cand_s[:, P * t : P * (t + 1)],
                rhs=zw[:].bitcast(FP8X4),
                rhs_scale=zs[:],
                start=True,
                stop=True,
            )
            if t == 0:
                nc.scalar.activation(rows[t][:, :S], bank[:], ACT.Copy, scale=SCORE_SCALE)
            else:
                nc.vector.tensor_scalar_mul(rows[t][:, :S], bank[:], SCORE_SCALE)

        ga, gb, pa, pb, up, res = [row_tiles(name) for name in ("ga", "gb", "pa", "pb", "up", "res")]
        ri = [sb.tile([P, HALF, PACK], BF16, name=f"ri_{h}", align_bytes=64) for h in range(2)]
        rw = sb.tile([P, S], U32, name="rw", align_bytes=64)
        rs = sb.tile([P, S], U8, name="rs", align_bytes=64)
        out_rows = out_0.rearrange("(p t) j -> p t j", t=PACK)
        out_words = out_1[0].rearrange("p c r -> p (c r)").bitcast(I32)

        def differences(t, cols):
            nc.scalar.activation(gb[:, t, cols], rows[t][:].indirect(entries(n4_sb, cols)), ACT.Copy)
            nc.scalar.activation(ga[:, t, cols], rows[t][:].indirect(entries(n3_sb, cols)), ACT.Copy)
            nc.vector.tensor_tensor(pb[:, t, cols], gb[:, t, cols], rows[t][:, cols], ALU.subtract)
            nc.vector.tensor_tensor(pa[:, t, cols], rows[t][:, cols], ga[:, t, cols], ALU.subtract)

        def clamp_above(t, cols):
            nc.vector.scalar_tensor_tensor(up[:, t, cols], pa[:, t, cols], 0.0, pb[:, t, cols], ALU.max, ALU.min)

        def clamp_below(t, cols):
            nc.vector.scalar_tensor_tensor(res[:, t, cols], pa[:, t, cols], 0.0, up[:, t, cols], ALU.min, ALU.max)

        def quantise_result(h, engine_copy):
            weave(engine_copy, ri[h][:], res[:, :, halves[h]])
            nc.vector.quantize_mx(out=rw[:, halves[h]].bitcast(FP8X4), scales=rs[:, halves[h]], in_=ri[h][:].rearrange("p j t -> p (j t)"))

        differences(*pieces[0])
        for before, piece in zip(pieces, pieces[1:]):
            clamp_above(*before)
            differences(*piece)
            clamp_below(*before)
            if before[0] == last - 1:
                nc.sync.dma_start(out_rows[:, :last, :], res[:, :last, :])
        clamp_above(*pieces[-1])
        quantise_result(0, nc.scalar.copy)
        clamp_below(*pieces[-1])
        nc.sync.dma_start(out_rows[:, last, :], res[:, last, :])
        quantise_result(1, nc.vector.tensor_copy)
        nc.sync.dma_start(out_words, rw[:].bitcast(I32))
        for q in range(P // QUADRANT):
            queue = nc.scalar if q % 2 == 0 else nc.sync
            queue.dma_start(out_2[0, 4 * q : 4 * q + 4, :].bitcast(I32), rs[QUADRANT * q : QUADRANT * q + 4, :].bitcast(I32))
